import numpy as np
import ml_dtypes


def mxq(x, axis, fmt="e4m3"):
    dtype, down = {"e4m3": (ml_dtypes.float8_e4m3fn, 7), "e5m2": (ml_dtypes.float8_e5m2, 14)}[fmt]
    v = np.moveaxis(np.asarray(x, np.float32).astype(ml_dtypes.bfloat16).astype(np.float64), axis, -1)
    blocks = v.reshape(v.shape[:-1] + (-1, 32))
    amax = np.abs(blocks).max(-1, keepdims=True)
    byte = np.maximum(np.where(amax > 0, np.frexp(amax)[1] - 1 + 127, 0) - down, 1)
    scale = np.exp2(byte - 127.0)
    codes = (blocks / scale).astype(np.float32).astype(dtype).astype(np.float64)
    return np.moveaxis((codes * scale).reshape(v.shape), -1, axis)


WIDE = False


def mx_kscale(k):
    if not WIDE:
        return np.ones(k)
    levels = np.array([10, -10, 5, -5, 0])
    if k % 512:
        return np.exp2(np.random.permutation(np.resize(levels, k // 32))).repeat(32)
    a = np.empty((k // 512, 16))
    for p in range(k // 512):
        a[p, :8] = np.random.permutation(np.resize(levels, 8))
        for g in range(8):
            far = levels[np.abs(levels - a[p, g]) >= 10]
            a[p, g + 8] = far[np.random.randint(len(far))]
    return np.exp2(a.ravel()).repeat(32)


def f64(x):
    return np.asarray(x).astype(np.float64)


def striped(idx):
    return np.tile(np.asarray(idx).reshape(-1, 16).T, (8, 1)).astype(np.uint16)


def unstriped(offs):
    return offs[:16].T.reshape(-1).astype(np.int64)


def striped8(idx):
    return np.asarray(idx).reshape(8, -1, 16).transpose(0, 2, 1).reshape(128, -1).astype(np.uint16)


def unstriped8(offs):
    return offs.reshape(8, 16, -1).transpose(0, 2, 1).reshape(8, -1).astype(np.int64)


def pick8(x, idx, run):
    r = np.arange(len(x))
    return x[r[:, None], idx[r % (8 * run) // run]]


E2M1 = np.array([0.0, 0.5, 1.0, 1.5, 2.0, 3.0, 4.0, 6.0, -0.0, -0.5, -1.0, -1.5, -2.0, -3.0, -4.0, -6.0])


def pack_weight(w, fmt):
    k, n = w.shape
    w = f64(np.asarray(w, np.float32).astype(ml_dtypes.bfloat16)).reshape(k // 32, 32, n)
    amax = np.abs(w).max(1)
    if fmt == "e4m3":
        byte = np.frexp(amax)[1] - 1 + 127 - 7
    else:
        mant, ex = np.frexp(amax / 6.0)
        byte = np.where(mant > 0.5, ex, ex - 1) + 127
    byte = np.clip(np.where(amax > 0, byte, 1), 1, 254)
    scaled = (w * np.exp2(127.0 - byte)[:, None, :]).reshape(k, n).astype(np.float32)
    by_word = np.ascontiguousarray(scaled.reshape(k // 512, 128, 4, n).transpose(0, 1, 3, 2))
    if fmt == "e4m3":
        words = by_word.astype(ml_dtypes.float8_e4m3fn).view(np.uint8)
    else:
        c = by_word.astype(ml_dtypes.float4_e2m1fn).view(np.uint8) & 0xF
        words = (c[..., 0::2] | (c[..., 1::2] << 4)).reshape(k // 512, 128, 2 * n)
    return np.ascontiguousarray(words), np.ascontiguousarray(byte.astype(np.uint8).reshape(k // 512, 16, n))


def unpack_weight(words, scales, fmt):
    g, _, n = scales.shape
    words = np.ascontiguousarray(words).reshape(g, 128, n, -1)
    if fmt == "e4m3":
        vals = words.view(ml_dtypes.float8_e4m3fn).astype(np.float64)
    else:
        nib = np.empty((g, 128, n, 4), np.uint8)
        nib[..., 0::2] = words & 0xF
        nib[..., 1::2] = words >> 4
        vals = E2M1[nib]
    vals = vals * np.repeat(np.exp2(scales.astype(np.float64) - 127.0), 8, axis=1)[..., None]
    return vals.transpose(0, 1, 3, 2).reshape(g * 512, n)


def sgn(shape):
    return np.random.uniform(0.5, 2.0, shape) * np.where(np.random.standard_normal(shape) < 0, -1.0, 1.0)


K, J, R, T, F, O, N, S, U, E = 512, 512, 512, 2048, 1024, 256, 256, 1024, 128, 512


def setup_inputs():
    n = np.random.standard_normal
    idx = np.stack([np.random.permutation(T)[:J] for _ in range(8)])
    idx2 = np.random.permutation(F)[:R]
    idx3 = np.stack([np.random.permutation(J)[:O] for _ in range(8)])
    idx4 = np.stack([np.random.permutation(J)[:O] for _ in range(8)])
    idx5 = np.stack([np.random.permutation(S)[:N] for _ in range(8)])
    idx6 = np.stack([np.random.permutation(O)[:U] for _ in range(8)])
    idx7 = np.stack([np.random.permutation(E)[:U] for _ in range(8)])
    fk = mx_kscale(K)
    fr = mx_kscale(R)
    tr = np.ones(F)
    tr[idx2] = fr
    wtp = pack_weight(n((K, F)) * 1 / np.sqrt(K) / fk[:, None] * tr, "e4m3")
    return {
        "ta": (np.random.randint(-7, 8, (K, T)).astype(np.float64)).astype(np.float32),
        "ga": ((np.random.randint(8, 25, (K, 1)) / 64.0) * fk[:, None]).astype(np.float32),
        "wt_words": wtp[0],
        "wt_scales": wtp[1],
        "sa": (np.random.uniform(0.5, 1.6, (R, 1))).astype(np.float32),
        "sb": (np.random.uniform(0.5, 1.6, (R, 1))).astype(np.float32),
        "va": (np.random.randint(-7, 8, (R, S)).astype(np.float64)).astype(np.float32),
        "ea": ((np.random.randint(8, 25, (R, 1)) / 1024.0) / fr[:, None]).astype(np.float32),
        "so": (sgn((N, 1))).astype(np.float32),
        "offs": striped8(idx),
        "offs2": striped(idx2),
        "offs3": striped8(idx3),
        "offs4": striped8(idx4),
        "offs5": striped8(idx5),
        "offs6": striped8(idx6),
        "offs7": striped8(idx7),
    }


def reference(ta, ga, wt_words, wt_scales, sa, sb, va, ea, so, offs, offs2, offs3, offs4, offs5, offs6, offs7):
    idx = unstriped8(offs)
    idx2 = unstriped(offs2)
    idx3 = unstriped8(offs3)
    idx4 = unstriped8(offs4)
    idx5 = unstriped8(offs5)
    idx6 = unstriped8(offs6)
    idx7 = unstriped8(offs7)
    wtu = unpack_weight(wt_words, wt_scales, "e4m3")
    xc = pick8(f64(ta), idx, 64) * f64(ga)
    wtidx2g = wtu[:, idx2]
    xcq = mxq(xc, 0, "e4m3")
    a = wtidx2g.T @ xcq
    hid = np.maximum(pick8(a, idx3, 64) * f64(sa), pick8(a, idx4, 64) * f64(sb))
    vc = pick8(f64(va), idx5, 64) * f64(ea)
    vcq = mxq(vc, 0, "e4m3")
    hidq = mxq(hid, 0, "e4m3")
    p = vcq.T @ hidq
    m0 = pick8(p, idx6, 16) * f64(so)
    y = np.zeros((N, E))
    y[np.arange(N)[:, None], idx7[np.arange(N) % 128 // 16]] = m0
    return y

@@ -1,0 +1,184 @@
+from contextlib import ExitStack
+
+import concourse.mybir as mybir
+
+F32 = mybir.dt.float32
+BF16 = mybir.dt.bfloat16
+I32 = mybir.dt.int32
+U32 = mybir.dt.uint32
+U16 = mybir.dt.uint16
+U8 = mybir.dt.uint8
+FP8X4 = mybir.dt.float8_e4m3fn_x4
+COPY = mybir.ActivationFunctionType.Copy
+MAX = mybir.AluOpType.max
+
+K, J, R, T, F, O, N, S, U, E = 512, 512, 512, 2048, 1024, 256, 256, 1024, 128, 512
+FLOPS = 2 * K * R * J + 2 * R * N * O
+
+P = 128
+PACK = 4
+HJ = J // 2
+HO = O // 2
+VSHARE = 512
+
+
+def tile_picked_codes_store_one_grouppair_codes_posted_kernel(
+    tc, ta, ga, wt_words, wt_scales, sa, sb, va, ea, so, offs, offs2, offs3, offs4, offs5, offs6, offs7, out
+):
+    nc = tc.nc
+    with ExitStack() as ctx:
+        keep = ctx.enter_context(tc.tile_pool(name="keep", bufs=1))
+        psum = ctx.enter_context(tc.psum_pool(name="psum", bufs=1))
+
+        def load_list(src, name):
+            dst = keep.tile([P, src.shape[1]], U16, name=name)
+            nc.sync.dma_start(dst[:], src)
+            return dst
+
+        def load_factors(src, name):
+            dst = keep.tile([P, PACK], F32, name=name)
+            nc.sync.dma_start(dst[:], src.rearrange("(p t) o -> p (t o)", t=PACK))
+            return dst
+
+        def load_rows(src, t, name):
+            dst = keep.tile([P, src.shape[1]], F32, name=name)
+            nc.sync.dma_start(dst[:], src.rearrange("(p t) c -> p t c", t=PACK)[:, t, :])
+            return dst
+
+        ta_sb = [load_rows(ta, 0, "ta0")]
+        l1 = load_list(offs, "l1")
+        ga_sb = load_factors(ga, "ga_sb")
+        w_win = keep.tile([P, F], U32, name="w_win")
+        nc.sync.dma_start(w_win[:].bitcast(I32), wt_words[0].rearrange("p c t -> p (c t)").bitcast(I32))
+        l2 = load_list(offs2, "l2")
+        s_stage = keep.tile([P, 2, F // 4], I32, name="s_stage")
+        for half in range(2):
+            nc.sync.dma_start(
+                s_stage[64 * half : 64 * half + 4, :, :],
+                wt_scales[0][8 * half : 8 * half + 8, :].bitcast(I32).rearrange("(q i) c -> i q c", q=2),
+            )
+        for t in range(1, PACK):
+            ta_sb.append(load_rows(ta, t, "ta%d" % t))
+        l5 = load_list(offs5, "l5")
+        ea_sb = load_factors(ea, "ea_sb")
+        va_sb = [load_rows(va, t, "va%d" % t) for t in range(2)]
+        l3 = load_list(offs3, "l3")
+        l4 = load_list(offs4, "l4")
+        sa_sb = load_factors(sa, "sa_sb")
+        sb_sb = load_factors(sb, "sb_sb")
+        for t in range(2, PACK):
+            va_sb.append(load_rows(va, t, "va%d" % t))
+        l6 = load_list(offs6, "l6")
+        l7 = load_list(offs7, "l7")
+        so_sb = keep.tile([P, N // P], F32, name="so_sb")
+        with nc.allow_non_contiguous_dma(reason="one value a partition and tile"):
+            nc.sync.dma_start(so_sb[:], so.rearrange("(i p) o -> p (i o)", p=P))
+
+        s_win = keep.tile([P, F], U8, name="s_win")
+        nc.vector.memset(s_win[:].bitcast(I32), 0)
+        pages = [keep.tile([P, E], F32, name="page%d" % i) for i in range(N // P)]
+        for page in pages:
+            nc.vector.memset(page[:], 0.0)
+
+        w_got = keep.tile([P, R], U32, name="w_got")
+        nc.vector.tensor_copy(w_got[:], w_win[:].indirect(l2[:]))
+        for q in range(4):
+            src = 64 * (q // 2)
+            nc.vector.tensor_copy(s_win[32 * q : 32 * q + 4, :].bitcast(I32), s_stage[src : src + 4, q % 2, :])
+        w_q = keep.tile([P, R], U32, name="w_q", align_bytes=64)
+        nc.vector.tensor_copy(
+            w_q[:].rearrange("p (t m) -> p t m", t=PACK), w_got[:].rearrange("p (m t) -> p t m", t=PACK)
+        )
+        s_got = keep.tile([P, R], U8, name="s_got")
+        nc.vector.tensor_copy(s_got[:], s_win[:].indirect(l2[:]))
+        w_s = keep.tile([P, R], U8, name="w_s", align_bytes=64)
+        nc.vector.tensor_copy(
+            w_s[:].rearrange("p (t m) -> p t m", t=PACK), s_got[:].rearrange("p (m t) -> p t m", t=PACK)
+        )
+
+        xc_il = keep.tile([P, J, PACK], BF16, name="xc_il", align_bytes=64)
+        for t in range(PACK):
+            xc_t = keep.tile([P, J], BF16, name="xc%d" % t)
+            nc.scalar.activation(xc_t[:], ta_sb[t][:].indirect(l1[:]), COPY, scale=ga_sb[:, t : t + 1])
+            nc.vector.tensor_copy(xc_il[:, 0:HJ, t], xc_t[:, 0:HJ])
+            nc.vector.tensor_copy(xc_il[:, HJ:VSHARE, t], xc_t[:, HJ:VSHARE])
+        x_q = keep.tile([P, J], U32, name="x_q", align_bytes=64)
+        x_s = keep.tile([P, J], U8, name="x_s", align_bytes=64)
+        for h in range(2):
+            cols = slice(h * HJ, (h + 1) * HJ)
+            nc.vector.quantize_mx(
+                out=x_q[:, cols].bitcast(FP8X4), scales=x_s[:, cols], in_=xc_il[:, cols, :].rearrange("p c t -> p (c t)")
+            )
+
+        def product(dst, lq, ls, lcols, rq, rs, rcols):
+            nc.tensor.matmul_mx(
+                out=dst,
+                lhsT=lq[:, lcols].bitcast(FP8X4),
+                lhsT_scale=ls[:, lcols],
+                rhs=rq[:, rcols].bitcast(FP8X4),
+                rhs_scale=rs[:, rcols],
+                start=True,
+                stop=True,
+            )
+
+        a_sb = [keep.tile([P, J], F32, name="a%d" % t) for t in range(PACK)]
+        for h in range(2):
+            cols = slice(h * HJ, (h + 1) * HJ)
+            acc = psum.tile([P, HJ], F32, name="acc_half", tag="bank%d" % h)
+            product(acc[:], w_q, w_s, slice(0, P), x_q, x_s, cols)
+            nc.scalar.copy(a_sb[0][:, cols], acc[:])
+        for t in range(1, PACK):
+            acc = psum.tile([P, J], F32, name="acc_full", tag="bank%d" % (t + 1))
+            product(acc[:], w_q, w_s, slice(t * P, (t + 1) * P), x_q, x_s, slice(0, J))
+            nc.vector.tensor_copy(a_sb[t][:], acc[:])
+
+        hid_il = keep.tile([P, O, PACK], BF16, name="hid_il", align_bytes=64)
+        hid_pl = keep.tile([P, PACK - 1, O], BF16, name="hid_pl")
+        g3 = [keep.tile([P, O], F32, name="g3_%d" % t) for t in range(PACK)]
+        g4 = [keep.tile([P, O], F32, name="g4_%d" % t) for t in range(PACK)]
+        for t in range(PACK - 1):
+            nc.scalar.activation(g3[t][:], a_sb[t][:].indirect(l3[:]), COPY, scale=sa_sb[:, t : t + 1])
+            nc.scalar.activation(g4[t][:], a_sb[t][:].indirect(l4[:]), COPY, scale=sb_sb[:, t : t + 1])
+            nc.vector.tensor_tensor(hid_pl[:, t, :], g3[t][:], g4[t][:], MAX)
+        nc.vector.tensor_copy(hid_il[:, :, 0 : PACK - 1], hid_pl[:].rearrange("p t o -> p o t"))
+
+        vc_pl = keep.tile([P, PACK, N], BF16, name="vc_pl")
+        for t in range(PACK):
+            nc.scalar.activation(vc_pl[:, t, :], va_sb[t][:].indirect(l5[:]), COPY, scale=ea_sb[:, t : t + 1])
+        vc_il = keep.tile([P, N, PACK], BF16, name="vc_il", align_bytes=64)
+        nc.vector.tensor_copy(vc_il[:], vc_pl[:].rearrange("p t n -> p n t"))
+        v_q = keep.tile([P, N], U32, name="v_q", align_bytes=64)
+        v_s = keep.tile([P, N], U8, name="v_s", align_bytes=64)
+        nc.vector.quantize_mx(out=v_q[:].bitcast(FP8X4), scales=v_s[:], in_=vc_il[:].rearrange("p c t -> p (c t)"))
+
+        last = PACK - 1
+        for h in range(2):
+            cols = slice(h * HO, (h + 1) * HO)
+            lcols = slice(h * HO // 16, (h + 1) * HO // 16)
+            nc.scalar.activation(g3[last][:, cols], a_sb[last][:].indirect(l3[:, lcols]), COPY, scale=sa_sb[:, last:PACK])
+            nc.scalar.activation(g4[last][:, cols], a_sb[last][:].indirect(l4[:, lcols]), COPY, scale=sb_sb[:, last:PACK])
+            nc.vector.tensor_tensor(hid_il[:, cols, last], g3[last][:, cols], g4[last][:, cols], MAX)
+        h_q = keep.tile([P, O], U32, name="h_q", align_bytes=64)
+        h_s = keep.tile([P, O], U8, name="h_s", align_bytes=64)
+        for h in range(2):
+            cols = slice(h * HO, (h + 1) * HO)
+            nc.vector.quantize_mx(
+                out=h_q[:, cols].bitcast(FP8X4), scales=h_s[:, cols], in_=hid_il[:, cols, :].rearrange("p c t -> p (c t)")
+            )
+
+        p_sb = [keep.tile([P, O], F32, name="p%d" % i) for i in range(N // P)]
+        p_banks = ("bank5", "bank6", "bank7", "bank0")
+        for h in range(2):
+            cols = slice(h * HO, (h + 1) * HO)
+            for i in range(N // P):
+                acc = psum.tile([P, HO], F32, name="acc_p", tag=p_banks[2 * h + i])
+                product(acc[:], v_q, v_s, slice(i * P, (i + 1) * P), h_q, h_s, cols)
+                if i == 0:
+                    nc.scalar.copy(p_sb[i][:, cols], acc[:])
+                else:
+                    nc.vector.tensor_copy(p_sb[i][:, cols], acc[:])
+        for i in range(N // P):
+            m0 = keep.tile([P, U], F32, name="m0_%d" % i)
+            nc.scalar.activation(m0[:], p_sb[i][:].indirect(l6[:]), COPY, scale=so_sb[:, i : i + 1])
+            nc.vector.tensor_copy(pages[i][:].indirect(l7[:]), m0[:])
+            nc.sync.dma_start(out[i * P : (i + 1) * P, :], pages[i][:])

@@ -45,29 +45,27 @@ def tile_picked_codes_store_one_grouppair_codes_posted_kernel(
             nc.sync.dma_start(dst[:], src.rearrange("(p t) c -> p t c", t=PACK)[:, t, :])
             return dst
 
-        ta_sb = [load_rows(ta, 0, "ta0")]
-        l1 = load_list(offs, "l1")
-        ga_sb = load_factors(ga, "ga_sb")
         w_win = keep.tile([P, F], U32, name="w_win")
         nc.sync.dma_start(w_win[:].bitcast(I32), wt_words[0].rearrange("p c t -> p (c t)").bitcast(I32))
         l2 = load_list(offs2, "l2")
-        s_stage = keep.tile([P, 2, F // 4], I32, name="s_stage")
-        for half in range(2):
-            nc.sync.dma_start(
-                s_stage[64 * half : 64 * half + 4, :, :],
-                wt_scales[0][8 * half : 8 * half + 8, :].bitcast(I32).rearrange("(q i) c -> i q c", q=2),
-            )
-        for t in range(1, PACK):
+        s_stage = keep.tile([P, F // 4], I32, name="s_stage")
+        for i in range(4):
+            nc.sync.dma_start(s_stage[i:P:32, :], wt_scales[0].bitcast(I32).rearrange("(q i) c -> i q c", i=4)[i])
+        ta_sb = [load_rows(ta, 0, "ta0")]
+        l1 = load_list(offs, "l1")
+        ga_sb = load_factors(ga, "ga_sb")
+        ta_sb.append(load_rows(ta, 1, "ta1"))
+        for t in range(2, PACK):
             ta_sb.append(load_rows(ta, t, "ta%d" % t))
         l5 = load_list(offs5, "l5")
         ea_sb = load_factors(ea, "ea_sb")
-        va_sb = [load_rows(va, t, "va%d" % t) for t in range(2)]
+        va_sb = [load_rows(va, t, "va%d" % t) for t in range(3)]
         l3 = load_list(offs3, "l3")
-        l4 = load_list(offs4, "l4")
         sa_sb = load_factors(sa, "sa_sb")
-        sb_sb = load_factors(sb, "sb_sb")
-        for t in range(2, PACK):
+        for t in range(3, PACK):
             va_sb.append(load_rows(va, t, "va%d" % t))
+        l4 = load_list(offs4, "l4")
+        sb_sb = load_factors(sb, "sb_sb")
         l6 = load_list(offs6, "l6")
         l7 = load_list(offs7, "l7")
         so_sb = keep.tile([P, N // P], F32, name="so_sb")
@@ -83,8 +81,7 @@ def tile_picked_codes_store_one_grouppair_codes_posted_kernel(
         w_got = keep.tile([P, R], U32, name="w_got")
         nc.vector.tensor_copy(w_got[:], w_win[:].indirect(l2[:]))
         for q in range(4):
-            src = 64 * (q // 2)
-            nc.vector.tensor_copy(s_win[32 * q : 32 * q + 4, :].bitcast(I32), s_stage[src : src + 4, q % 2, :])
+            nc.vector.tensor_copy(s_win[32 * q : 32 * q + 4, :].bitcast(I32), s_stage[32 * q : 32 * q + 4, :])
         w_q = keep.tile([P, R], U32, name="w_q", align_bytes=64)
         nc.vector.tensor_copy(
             w_q[:].rearrange("p (t m) -> p t m", t=PACK), w_got[:].rearrange("p (m t) -> p t m", t=PACK)
@@ -126,25 +123,26 @@ def tile_picked_codes_store_one_grouppair_codes_posted_kernel(
             cols = slice(h * HJ, (h + 1) * HJ)
             acc = psum.tile([P, HJ], F32, name="acc_half", tag="bank%d" % h)
             product(acc[:], w_q, w_s, slice(0, P), x_q, x_s, cols)
-            nc.scalar.copy(a_sb[0][:, cols], acc[:])
+            nc.vector.tensor_copy(a_sb[0][:, cols], acc[:])
         for t in range(1, PACK):
             acc = psum.tile([P, J], F32, name="acc_full", tag="bank%d" % (t + 1))
             product(acc[:], w_q, w_s, slice(t * P, (t + 1) * P), x_q, x_s, slice(0, J))
             nc.vector.tensor_copy(a_sb[t][:], acc[:])
 
-        hid_il = keep.tile([P, O, PACK], BF16, name="hid_il", align_bytes=64)
-        hid_pl = keep.tile([P, PACK - 1, O], BF16, name="hid_pl")
-        g3 = [keep.tile([P, O], F32, name="g3_%d" % t) for t in range(PACK)]
-        g4 = [keep.tile([P, O], F32, name="g4_%d" % t) for t in range(PACK)]
-        for t in range(PACK - 1):
-            nc.scalar.activation(g3[t][:], a_sb[t][:].indirect(l3[:]), COPY, scale=sa_sb[:, t : t + 1])
-            nc.scalar.activation(g4[t][:], a_sb[t][:].indirect(l4[:]), COPY, scale=sb_sb[:, t : t + 1])
-            nc.vector.tensor_tensor(hid_pl[:, t, :], g3[t][:], g4[t][:], MAX)
-        nc.vector.tensor_copy(hid_il[:, :, 0 : PACK - 1], hid_pl[:].rearrange("p t o -> p o t"))
-
         vc_pl = keep.tile([P, PACK, N], BF16, name="vc_pl")
         for t in range(PACK):
             nc.scalar.activation(vc_pl[:, t, :], va_sb[t][:].indirect(l5[:]), COPY, scale=ea_sb[:, t : t + 1])
+
+        hid_il = keep.tile([P, O, PACK], BF16, name="hid_il", align_bytes=64)
+        g3_tags = ("pair0", "pair1", "a0", "a1")
+        pairs = [keep.tile([P, 2, O], F32, name="pair%d" % t, tag=g3_tags[t]) for t in range(PACK)]
+        g3 = [pair[:, 0, :] for pair in pairs]
+        g4 = [pair[:, 1, :] for pair in pairs]
+        for t in range(PACK - 1):
+            nc.scalar.activation(g3[t], a_sb[t][:].indirect(l3[:]), COPY, scale=sa_sb[:, t : t + 1])
+            nc.scalar.activation(g4[t], a_sb[t][:].indirect(l4[:]), COPY, scale=sb_sb[:, t : t + 1])
+            nc.vector.tensor_tensor(hid_il[:, :, t], g3[t], g4[t], MAX)
+
         vc_il = keep.tile([P, N, PACK], BF16, name="vc_il", align_bytes=64)
         nc.vector.tensor_copy(vc_il[:], vc_pl[:].rearrange("p t n -> p n t"))
         v_q = keep.tile([P, N], U32, name="v_q", align_bytes=64)
@@ -152,10 +150,10 @@ def tile_picked_codes_store_one_grouppair_codes_posted_kernel(
         nc.vector.quantize_mx(out=v_q[:].bitcast(FP8X4), scales=v_s[:], in_=vc_il[:].rearrange("p c t -> p (c t)"))
 
         last = PACK - 1
+        nc.scalar.activation(g3[last], a_sb[last][:].indirect(l3[:]), COPY, scale=sa_sb[:, last:PACK])
         for h in range(2):
             cols = slice(h * HO, (h + 1) * HO)
             lcols = slice(h * HO // 16, (h + 1) * HO // 16)
-            nc.scalar.activation(g3[last][:, cols], a_sb[last][:].indirect(l3[:, lcols]), COPY, scale=sa_sb[:, last:PACK])
             nc.scalar.activation(g4[last][:, cols], a_sb[last][:].indirect(l4[:, lcols]), COPY, scale=sb_sb[:, last:PACK])
             nc.vector.tensor_tensor(hid_il[:, cols, last], g3[last][:, cols], g4[last][:, cols], MAX)
         h_q = keep.tile([P, O], U32, name="h_q", align_bytes=64)
@@ -167,16 +165,14 @@ def tile_picked_codes_store_one_grouppair_codes_posted_kernel(
             )
 
         p_sb = [keep.tile([P, O], F32, name="p%d" % i) for i in range(N // P)]
-        p_banks = ("bank5", "bank6", "bank7", "bank0")
         for h in range(2):
             cols = slice(h * HO, (h + 1) * HO)
-            for i in range(N // P):
-                acc = psum.tile([P, HO], F32, name="acc_p", tag=p_banks[2 * h + i])
-                product(acc[:], v_q, v_s, slice(i * P, (i + 1) * P), h_q, h_s, cols)
-                if i == 0:
-                    nc.scalar.copy(p_sb[i][:, cols], acc[:])
-                else:
-                    nc.vector.tensor_copy(p_sb[i][:, cols], acc[:])
+            acc = psum.tile([P, HO], F32, name="acc_p0", tag="bank%d" % (5 + h))
+            product(acc[:], v_q, v_s, slice(0, P), h_q, h_s, cols)
+            nc.scalar.copy(p_sb[0][:, cols], acc[:])
+        acc = psum.tile([P, O], F32, name="acc_p1", tag="bank7")
+        product(acc[:], v_q, v_s, slice(P, N), h_q, h_s, slice(0, O))
+        nc.vector.tensor_copy(p_sb[1][:], acc[:])
         for i in range(N // P):
             m0 = keep.tile([P, U], F32, name="m0_%d" % i)
             nc.scalar.activation(m0[:], p_sb[i][:].indirect(l6[:]), COPY, scale=so_sb[:, i : i + 1])

from contextlib import ExitStack

import concourse.mybir as mybir

F32 = mybir.dt.float32
BF16 = mybir.dt.bfloat16
I32 = mybir.dt.int32
U32 = mybir.dt.uint32
U16 = mybir.dt.uint16
U8 = mybir.dt.uint8
FP8X4 = mybir.dt.float8_e4m3fn_x4
COPY = mybir.ActivationFunctionType.Copy
MAX = mybir.AluOpType.max

K, J, R, T, F, O, N, S, U, E = 512, 512, 512, 2048, 1024, 256, 256, 1024, 128, 512
FLOPS = 2 * K * R * J + 2 * R * N * O

P = 128
PACK = 4
HJ = J // 2
HO = O // 2
VSHARE = 512


def tile_picked_codes_store_one_grouppair_codes_posted_kernel(
    tc, ta, ga, wt_words, wt_scales, sa, sb, va, ea, so, offs, offs2, offs3, offs4, offs5, offs6, offs7, out
):
    nc = tc.nc
    with ExitStack() as ctx:
        keep = ctx.enter_context(tc.tile_pool(name="keep", bufs=1))
        psum = ctx.enter_context(tc.psum_pool(name="psum", bufs=1))

        def load_list(src, name):
            dst = keep.tile([P, src.shape[1]], U16, name=name)
            nc.sync.dma_start(dst[:], src)
            return dst

        def load_factors(src, name):
            dst = keep.tile([P, PACK], F32, name=name)
            nc.sync.dma_start(dst[:], src.rearrange("(p t) o -> p (t o)", t=PACK))
            return dst

        def load_rows(src, t, name):
            dst = keep.tile([P, src.shape[1]], F32, name=name)
            nc.sync.dma_start(dst[:], src.rearrange("(p t) c -> p t c", t=PACK)[:, t, :])
            return dst

        w_win = keep.tile([P, F], U32, name="w_win")
        nc.sync.dma_start(w_win[:].bitcast(I32), wt_words[0].rearrange("p c t -> p (c t)").bitcast(I32))
        l2 = load_list(offs2, "l2")
        s_stage = keep.tile([P, F // 4], I32, name="s_stage")
        for i in range(4):
            nc.sync.dma_start(s_stage[i:P:32, :], wt_scales[0].bitcast(I32).rearrange("(q i) c -> i q c", i=4)[i])
        ta_sb = [load_rows(ta, 0, "ta0")]
        l1 = load_list(offs, "l1")
        ga_sb = load_factors(ga, "ga_sb")
        ta_sb.append(load_rows(ta, 1, "ta1"))
        for t in range(2, PACK):
            ta_sb.append(load_rows(ta, t, "ta%d" % t))
        l5 = load_list(offs5, "l5")
        ea_sb = load_factors(ea, "ea_sb")
        va_sb = [load_rows(va, t, "va%d" % t) for t in range(3)]
        l3 = load_list(offs3, "l3")
        sa_sb = load_factors(sa, "sa_sb")
        for t in range(3, PACK):
            va_sb.append(load_rows(va, t, "va%d" % t))
        l4 = load_list(offs4, "l4")
        sb_sb = load_factors(sb, "sb_sb")
        l6 = load_list(offs6, "l6")
        l7 = load_list(offs7, "l7")
        so_sb = keep.tile([P, N // P], F32, name="so_sb")
        with nc.allow_non_contiguous_dma(reason="one value a partition and tile"):
            nc.sync.dma_start(so_sb[:], so.rearrange("(i p) o -> p (i o)", p=P))

        s_win = keep.tile([P, F], U8, name="s_win")
        nc.vector.memset(s_win[:].bitcast(I32), 0)
        pages = [keep.tile([P, E], F32, name="page%d" % i) for i in range(N // P)]
        for page in pages:
            nc.vector.memset(page[:], 0.0)

        w_got = keep.tile([P, R], U32, name="w_got")
        nc.vector.tensor_copy(w_got[:], w_win[:].indirect(l2[:]))
        for q in range(4):
            nc.vector.tensor_copy(s_win[32 * q : 32 * q + 4, :].bitcast(I32), s_stage[32 * q : 32 * q + 4, :])
        w_q = keep.tile([P, R], U32, name="w_q", align_bytes=64)
        nc.vector.tensor_copy(
            w_q[:].rearrange("p (t m) -> p t m", t=PACK), w_got[:].rearrange("p (m t) -> p t m", t=PACK)
        )
        s_got = keep.tile([P, R], U8, name="s_got")
        nc.vector.tensor_copy(s_got[:], s_win[:].indirect(l2[:]))
        w_s = keep.tile([P, R], U8, name="w_s", align_bytes=64)
        nc.vector.tensor_copy(
            w_s[:].rearrange("p (t m) -> p t m", t=PACK), s_got[:].rearrange("p (m t) -> p t m", t=PACK)
        )

        xc_il = keep.tile([P, J, PACK], BF16, name="xc_il", align_bytes=64)
        for t in range(PACK):
            xc_t = keep.tile([P, J], BF16, name="xc%d" % t)
            nc.scalar.activation(xc_t[:], ta_sb[t][:].indirect(l1[:]), COPY, scale=ga_sb[:, t : t + 1])
            nc.vector.tensor_copy(xc_il[:, 0:HJ, t], xc_t[:, 0:HJ])
            nc.vector.tensor_copy(xc_il[:, HJ:VSHARE, t], xc_t[:, HJ:VSHARE])
        x_q = keep.tile([P, J], U32, name="x_q", align_bytes=64)
        x_s = keep.tile([P, J], U8, name="x_s", align_bytes=64)
        for h in range(2):
            cols = slice(h * HJ, (h + 1) * HJ)
            nc.vector.quantize_mx(
                out=x_q[:, cols].bitcast(FP8X4), scales=x_s[:, cols], in_=xc_il[:, cols, :].rearrange("p c t -> p (c t)")
            )

        def product(dst, lq, ls, lcols, rq, rs, rcols):
            nc.tensor.matmul_mx(
                out=dst,
                lhsT=lq[:, lcols].bitcast(FP8X4),
                lhsT_scale=ls[:, lcols],
                rhs=rq[:, rcols].bitcast(FP8X4),
                rhs_scale=rs[:, rcols],
                start=True,
                stop=True,
            )

        a_sb = [keep.tile([P, J], F32, name="a%d" % t) for t in range(PACK)]
        for h in range(2):
            cols = slice(h * HJ, (h + 1) * HJ)
            acc = psum.tile([P, HJ], F32, name="acc_half", tag="bank%d" % h)
            product(acc[:], w_q, w_s, slice(0, P), x_q, x_s, cols)
            nc.vector.tensor_copy(a_sb[0][:, cols], acc[:])
        for t in range(1, PACK):
            acc = psum.tile([P, J], F32, name="acc_full", tag="bank%d" % (t + 1))
            product(acc[:], w_q, w_s, slice(t * P, (t + 1) * P), x_q, x_s, slice(0, J))
            nc.vector.tensor_copy(a_sb[t][:], acc[:])

        vc_pl = keep.tile([P, PACK, N], BF16, name="vc_pl")
        for t in range(PACK):
            nc.scalar.activation(vc_pl[:, t, :], va_sb[t][:].indirect(l5[:]), COPY, scale=ea_sb[:, t : t + 1])

        hid_il = keep.tile([P, O, PACK], BF16, name="hid_il", align_bytes=64)
        g3_tags = ("pair0", "pair1", "a0", "a1")
        pairs = [keep.tile([P, 2, O], F32, name="pair%d" % t, tag=g3_tags[t]) for t in range(PACK)]
        g3 = [pair[:, 0, :] for pair in pairs]
        g4 = [pair[:, 1, :] for pair in pairs]
        for t in range(PACK - 1):
            nc.scalar.activation(g3[t], a_sb[t][:].indirect(l3[:]), COPY, scale=sa_sb[:, t : t + 1])
            nc.scalar.activation(g4[t], a_sb[t][:].indirect(l4[:]), COPY, scale=sb_sb[:, t : t + 1])
            nc.vector.tensor_tensor(hid_il[:, :, t], g3[t], g4[t], MAX)

        vc_il = keep.tile([P, N, PACK], BF16, name="vc_il", align_bytes=64)
        nc.vector.tensor_copy(vc_il[:], vc_pl[:].rearrange("p t n -> p n t"))
        v_q = keep.tile([P, N], U32, name="v_q", align_bytes=64)
        v_s = keep.tile([P, N], U8, name="v_s", align_bytes=64)
        nc.vector.quantize_mx(out=v_q[:].bitcast(FP8X4), scales=v_s[:], in_=vc_il[:].rearrange("p c t -> p (c t)"))

        last = PACK - 1
        nc.scalar.activation(g3[last], a_sb[last][:].indirect(l3[:]), COPY, scale=sa_sb[:, last:PACK])
        for h in range(2):
            cols = slice(h * HO, (h + 1) * HO)
            lcols = slice(h * HO // 16, (h + 1) * HO // 16)
            nc.scalar.activation(g4[last][:, cols], a_sb[last][:].indirect(l4[:, lcols]), COPY, scale=sb_sb[:, last:PACK])
            nc.vector.tensor_tensor(hid_il[:, cols, last], g3[last][:, cols], g4[last][:, cols], MAX)
        h_q = keep.tile([P, O], U32, name="h_q", align_bytes=64)
        h_s = keep.tile([P, O], U8, name="h_s", align_bytes=64)
        for h in range(2):
            cols = slice(h * HO, (h + 1) * HO)
            nc.vector.quantize_mx(
                out=h_q[:, cols].bitcast(FP8X4), scales=h_s[:, cols], in_=hid_il[:, cols, :].rearrange("p c t -> p (c t)")
            )

        p_sb = [keep.tile([P, O], F32, name="p%d" % i) for i in range(N // P)]
        for h in range(2):
            cols = slice(h * HO, (h + 1) * HO)
            acc = psum.tile([P, HO], F32, name="acc_p0", tag="bank%d" % (5 + h))
            product(acc[:], v_q, v_s, slice(0, P), h_q, h_s, cols)
            nc.scalar.copy(p_sb[0][:, cols], acc[:])
        acc = psum.tile([P, O], F32, name="acc_p1", tag="bank7")
        product(acc[:], v_q, v_s, slice(P, N), h_q, h_s, slice(0, O))
        nc.vector.tensor_copy(p_sb[1][:], acc[:])
        for i in range(N // P):
            m0 = keep.tile([P, U], F32, name="m0_%d" % i)
            nc.scalar.activation(m0[:], p_sb[i][:].indirect(l6[:]), COPY, scale=so_sb[:, i : i + 1])
            nc.vector.tensor_copy(pages[i][:].indirect(l7[:]), m0[:])
            nc.sync.dma_start(out[i * P : (i + 1) * P, :], pages[i][:])
